import numpy as np
CORES = [12,28,60,100,156,228]
N = 6
J, Q = 512, 2048
def entries(a): return a.T.reshape(-1)
def pack(v, P): return np.ascontiguousarray(np.asarray(v, np.int32).reshape(-1, P).T)
def split(rng, total, parts):
    c = np.sort(rng.integers(0, total + 1, parts - 1)); return np.diff(np.concatenate([[0], c, [total]]))
def lists(rng, how):
    s = np.concatenate([[0], rng.integers(1 - Q // 2, Q // 2 + 1, N - 1), [int(rng.integers(1 - Q // 2, 1))]])
    if how == "early": s[1:] = -Q; s[N] = -2 * Q
    if how == "late": s[1:] = Q; s[N] = 0
    if how == "long":
        z = int(rng.integers(1, N - 1)); s[1:z] = -rng.integers(1, Q, z - 1); s[z] = -Q; s[z + 1] = Q; s[z + 2:N] = rng.integers(1, Q, N - z - 2); s[N] = -int(rng.integers(0, Q - s[N - 1] + 1))
    if how == "sway":
        z = int(rng.integers(1, N - 2)); e = int(rng.integers(z + 1, N - 1)); s[1:] = -rng.integers(Q // 2 + 1, Q, N); s[z + 1:e + 1] = rng.integers(Q // 2 + 1, Q - 1, e - z); s[e + 1] = s[e] - Q; s[N] = s[N - 1] - Q + int(rng.integers(1, -s[N - 1]))
    tot = Q + np.diff(s)
    L = np.stack([split(rng, int(t), J) for t in tot])
    if how == "gaps":
        L = np.zeros((N, J), np.int64)
        for r in range(N): m = 1 if r & 1 else 8; L[r, 1 + rng.permutation(J - 2)[:m]] = split(rng, int(tot[r]), m)
    if how == "long":
        L = np.zeros((N, J), np.int64); L[np.arange(N), rng.integers(0, J, N)] = tot
    return {"ln": np.stack([pack(l, 16) for l in L])}
def setup_inputs(rng):
    return dict({"x": rng.standard_normal((N, 128, J), dtype=np.float32)}, **lists(rng, "uniform"))
def setup_inputs_early(rng):
    d = setup_inputs(rng); d.update(lists(rng, "early"))
    for k in ("x",): d[k] = (d[k].astype(np.float32) * 1048576.0).astype(d[k].dtype)
    return d
def setup_inputs_gaps(rng):
    d = setup_inputs(rng); d.update(lists(rng, "gaps"))
    for k in ("x",): d[k] = (d[k].astype(np.float32) * (1 / 1024.0)).astype(d[k].dtype)
    return d
def setup_inputs_late(rng):
    d = setup_inputs(rng); d.update(lists(rng, "late"))
    return d
def setup_inputs_long(rng):
    d = setup_inputs(rng); d.update(lists(rng, "long"))
    return d
def setup_inputs_sway(rng):
    d = setup_inputs(rng); d.update(lists(rng, "sway"))
    return d
def check_inputs(x):
    bad = []
    if x["ln"].min() < 0 or x["ln"].max() >= N * Q + 1: bad.append("ln out of range")
    if int(x["ln"].sum()) > N * Q: bad.append("the lengths come to more than N * Q")
    c = np.concatenate([[0], np.cumsum([int(a.sum()) for a in x["ln"]])])
    if any(c[r] < (r - 1) * Q or c[r + 1] > (r + 2) * Q for r in range(N)): bad.append("the sums of the lengths before or up to a rank leave their bounds")
    return bad
def reference(x, ln):
    got = np.concatenate([np.repeat(x[r], entries(ln[r]), axis=1) for r in range(N)], axis=1)[:, :N * Q]
    Y = np.zeros((128, N * Q), x.dtype); Y[:, :got.shape[1]] = got
    return {"y": np.stack([Y[:, Q * r:Q * r + Q] for r in range(N)])}

@@ -1,0 +1,308 @@
+from concourse.bass import DstId, RemoteDMATransfer
+from concourse.mybir import AluOpType as A, ActivationFunctionType as F
+
+N, J, Q = 6, 512, 2048
+SIM = 256
+WZ = 3 * J + 4
+
+SCRATCH = {
+    "lnd": ("dram", [2, 128, 2], "int32"),
+    "xd": ("dram", [2, 128, 256], "float32"),
+    "lnh": ("dram", [128, 2], "int32"),
+    "xh": ("dram", [128, 256], "float32"),
+    "Li": ("sbuf", [128, 4 * N], "int32"),
+    "win": ("sbuf", [128, WZ], "float32"),
+    "ni": ("sbuf", [128, 128], "int32"), "pi": ("sbuf", [128, 4], "int32"),
+    "bi": ("sbuf", [128, 128], "int32"), "ri": ("sbuf", [128, 128], "int32"),
+    "pbi": ("sbuf", [128, 4], "int32"), "pri": ("sbuf", [128, 4], "int32"),
+    "pb": ("sbuf", [128, 4], "float32"), "pr": ("sbuf", [128, 4], "float32"), "pf": ("sbuf", [128, 4], "float32"),
+    "MA": ("sbuf", [128, 128], "float32"), "MB": ("sbuf", [128, 128], "float32"), "MD": ("sbuf", [128, 128], "float32"),
+    "MC0": ("sbuf", [128, 128], "float32"), "MC": ("sbuf", [128, 128], "float32"),
+    "I16": ("sbuf", [128, 128], "float16"), "T0": ("sbuf", [128, 128], "float16"), "T2": ("sbuf", [128, 128], "float16"),
+    "iq": ("sbuf", [128, 128], "bfloat16"), "im": ("sbuf", [128, 128], "bfloat16"),
+    "oneh": ("sbuf", [128, 128], "float16"), "ones": ("sbuf", [128, 56], "float32"),
+    "Lf": ("sbuf", [128, 56], "float32"), "S": ("sbuf", [128, 56], "float32"),
+    "Abf": ("sbuf", [128, 24], "bfloat16"), "Ff": ("sbuf", [128, 24], "float32"), "Bf": ("sbuf", [128, 24], "float32"),
+    "OA": ("sbuf", [128, 12 * 128], "bfloat16"), "OB": ("sbuf", [128, 12 * 128], "bfloat16"),
+    "Hs": ("sbuf", [128, 128], "float16"), "H15": ("sbuf", [128, 128], "float16"),
+    "off": ("sbuf", [128, 128], "uint16"),
+    "yb": ("sbuf", [128, Q], "float32"),
+    "psE": ("psum", [128, 512], "float32"), "psH": ("psum", [128, 512], "float32"), "psC": ("psum", [128, 512], "float32"),
+}
+EV = ["e%d" % i for i in range(48)]
+SEMAPHORES = ["s_lnd", "s_xd", "s_li", "s_w", "s_yv", "s_ys", "ln_in", "x_in", "hl", "hx", "ls"] + EV
+
+
+def _bits(mask):
+    return [e for e in range(16) if (mask >> e) & 1]
+
+
+def _mask(engines):
+    return sum(1 << e for e in engines)
+
+
+def _lists_to(r):
+    return [d for d in range(N) if d != r and d >= r - 1]
+
+
+def _x_to(r):
+    return [d for d in (r - 1, r + 1) if 0 <= d < N]
+
+
+def _slot(r, d):
+    return (r - max(d - 1, 0)) * J
+
+
+def _helpers(r, T, topo):
+    me = T.cores[r]
+    far = [d for d in _lists_to(r) if not topo.may_write(me, T.cores[d])]
+    if not far:
+        return {}
+    chip = [c for c in range(SIM) if c != me and topo.host(c) == topo.host(me) and topo.chip(c) == topo.chip(me)
+            and all(topo.may_write(c, T.cores[d]) for d in far)]
+    own = [c for c in chip if topo.die(c) == topo.die(me)]
+    oth = [c for c in chip if topo.die(c) != topo.die(me)]
+    plan = {}
+    for k, d in enumerate(far):
+        plan[(d, 0)] = own[k]
+        plan[(d, 1)] = oth[k]
+    return plan
+
+
+def _xfer(topo, src_core, cores, engines, sem, src, dsts):
+    ids = []
+    for c in cores:
+        rid, pid = topo.addr(c, src_core)
+        ids.append(DstId(rid=rid, pnc=pid))
+    return RemoteDMATransfer(dst_ids=ids, dma_engine_mask=_mask(engines), remote_sem=sem, srcs=[src], dsts=dsts, alu_op=0)
+
+
+def _helper_program(g, core, T, topo, r, d, half):
+    dst = T.cores[d]
+    eng = _bits(topo.mask(core, dst))
+    n = 0
+    g.wait_ge(T.sem.hl, 1)
+    g.remote_dma_fused([_xfer(topo, core, [dst], eng, T.sem.ln_in, T.lnh[:],
+                              [T.Li[:, 4 * r + 2 * half:4 * r + 2 * half + 2]])], local_sem=T.sem.ls)
+    n += len(eng)
+    if d in _x_to(r):
+        g.wait_ge(T.sem.hx, len(_bits(topo.mask(T.cores[r], core))) // 2)
+        o = _slot(r, d) + 256 * half
+        g.remote_dma_fused([_xfer(topo, core, [dst], eng, T.sem.x_in, T.xh[:], [T.win[:, o:o + 256]])],
+                           local_sem=T.sem.ls)
+        n += len(eng)
+    g.wait_ge(T.sem.ls, n)
+
+
+def rank_program(g, core, T, topo):
+    s = T.rank_of(core)
+    if s is None:
+        for r in range(N):
+            for (d, half), c in _helpers(r, T, topo).items():
+                if c == core:
+                    _helper_program(g, core, T, topo, r, d, half)
+        return
+
+    plan = _helpers(s, T, topo)
+    far_x = [d for d in _x_to(s) if (d, 0) in plan]
+    near_x = [d for d in _x_to(s) if (d, 0) not in plan]
+    far_l = [d for d in _lists_to(s) if (d, 0) in plan]
+    near_l = [d for d in _lists_to(s) if (d, 0) not in plan]
+    lo, hi = max(s - 1, 0), min(s + 1, N - 1)
+    nw, nr = hi - lo + 1, hi + 1
+    own = _slot(s, s)
+    V, S, P = g.vector, g.scalar, g.tensor
+    free = [0]
+
+    def new(n):
+        free[0] += 1
+        return (T.sem[EV[free[0] - 1]], n)
+
+    def on(q, e):
+        q.wait_ge(e[0], e[1])
+
+    if far_l:
+        g.scalar.dma_start(T.lnd[:], T.ln[:]).then_inc(T.sem.s_lnd, 16)
+    if far_x:
+        g.sync.dma_start(T.xd[0], T.x[:, 0:256]).then_inc(T.sem.s_xd, 16)
+        g.scalar.dma_start(T.xd[1], T.x[:, 256:512]).then_inc(T.sem.s_xd, 16)
+    else:
+        g.sync.dma_start(T.win[:, own:own + J], T.x[:]).then_inc(T.sem.s_w, 16)
+    g.scalar.dma_start(T.Li[:, 4 * s:4 * s + 2], T.ln[0:8, :]).then_inc(T.sem.s_li, 16)
+    g.scalar.dma_start(T.Li[:, 4 * s + 2:4 * s + 4], T.ln[8:16, :]).then_inc(T.sem.s_li, 16)
+    if far_x:
+        g.sync.wait_ge(T.sem.s_xd, 32)
+        g.sync.dma_start(T.win[:, own:own + J], T.x[:]).then_inc(T.sem.s_w, 16)
+
+    e_io = new(2)
+    g.iota(T.ni[:, 0:128], [[1, 128]], 0, 0).then_inc(e_io[0], 1)
+    g.iota(T.pi[:, 0:1], [[0, 1]], 0, 1).then_inc(e_io[0], 1)
+    sent = 0
+    if far_l:
+        g.wait_ge(T.sem.s_lnd, 16)
+        eng = _bits(topo.mask(core, plan[(far_l[0], 0)]))
+        tr = []
+        for half in (0, 1):
+            cs = [plan[(d, half)] for d in far_l]
+            tr.append(_xfer(topo, core, cs, [eng[1 - half]], T.sem.hl, T.lnd[half], [T.lnh[:]] * len(cs)))
+        g.remote_dma_fused(tr, local_sem=T.sem.ls)
+        sent += 2
+    if far_x:
+        g.wait_ge(T.sem.s_xd, 32)
+        eng = _bits(topo.mask(core, plan[(far_x[0], 0)]))
+        tr = []
+        for half in (0, 1):
+            cs = [plan[(d, half)] for d in far_x]
+            tr.append(_xfer(topo, core, cs, eng[1 - half::2], T.sem.hx, T.xd[half], [T.xh[:]] * len(cs)))
+        g.remote_dma_fused(tr, local_sem=T.sem.ls)
+        sent += len(eng)
+    if near_l:
+        g.wait_ge(T.sem.s_li, 32)
+        eng = _bits(topo.mask(core, T.cores[near_l[0]]))
+        ap = T.Li[:, 4 * s:4 * s + 4]
+        g.remote_dma_fused([_xfer(topo, core, [T.cores[d] for d in near_l], eng, T.sem.ln_in, ap, [ap] * len(near_l))],
+                           local_sem=T.sem.ls)
+        sent += len(eng)
+    if near_x:
+        g.wait_ge(T.sem.s_w, 16)
+        eng = _bits(topo.mask(core, T.cores[near_x[0]]))
+        g.remote_dma_fused([_xfer(topo, core, [T.cores[d] for d in near_x], eng, T.sem.x_in, T.win[:, own:own + J],
+                                  [T.win[:, _slot(s, d):_slot(s, d) + J] for d in near_x])], local_sem=T.sem.ls)
+        sent += len(eng)
+
+    ln_all = x_all = 0
+    for r in range(N):
+        if r == s or s not in _lists_to(r):
+            continue
+        p = _helpers(r, T, topo)
+        from_cores = [p[(s, 0)], p[(s, 1)]] if (s, 0) in p else [T.cores[r]]
+        cnt = sum(len(_bits(topo.mask(c, core))) for c in from_cores)
+        ln_all += cnt
+        if s in _x_to(r):
+            x_all += cnt
+
+    e0 = new(3)
+    V.memset(T.Lf[:], 0.0).then_inc(e0[0], 1)
+    V.memset(T.ones[:], 1.0).then_inc(e0[0], 1)
+    V.memset(T.win[:, nw * J:nw * J + 4], 0.0).then_inc(e0[0], 1)
+    on(V, e_io)
+    e1 = new(6)
+    V.tensor_scalar(T.bi[:], T.ni[:], 15, None, A.bitwise_and).then_inc(e1[0], 1)
+    V.tensor_scalar(T.ri[:], T.ni[:], 4, None, A.arith_shift_right).then_inc(e1[0], 1)
+    V.tensor_scalar(T.pbi[:, 0:1], T.pi[:, 0:1], 15, None, A.bitwise_and).then_inc(e1[0], 1)
+    V.tensor_scalar(T.pri[:, 0:1], T.pi[:, 0:1], 4, None, A.arith_shift_right).then_inc(e1[0], 1)
+    V.tensor_scalar(T.iq[:], T.ni[:], 128.0, None, A.add).then_inc(e1[0], 1)
+    V.tensor_scalar(T.oneh[:], T.ni[:], 0.0, 1.0, A.mult, A.add).then_inc(e1[0], 1)
+    on(V, e1)
+    e2 = new(4)
+    V.tensor_copy(T.pb[:, 0:1], T.pbi[:, 0:1]).then_inc(e2[0], 1)
+    V.tensor_copy(T.pr[:, 0:1], T.pri[:, 0:1]).then_inc(e2[0], 1)
+    V.tensor_copy(T.pf[:, 0:1], T.pi[:, 0:1]).then_inc(e2[0], 1)
+    V.tensor_scalar(T.im[:], T.bi[:], 1.0 / 16, 1.0 / 32, A.mult, A.add).then_inc(e2[0], 1)
+    on(V, e2)
+    e3 = new(6)
+    V.tensor_scalar(T.MA[:], T.bi[:], T.pb[:, 0:1], 1.0 / 16, A.is_gt, A.mult).then_inc(e3[0], 1)
+    V.tensor_scalar(T.MB[:], T.bi[:], T.pb[:, 0:1], 1.0 / 16, A.is_equal, A.mult).then_inc(e3[0], 1)
+    V.tensor_scalar(T.MD[:], T.bi[:], T.pb[:, 0:1], 1.0 / 16, A.is_lt, A.mult).then_inc(e3[0], 1)
+    V.tensor_scalar(T.MC0[:], T.ri[:], T.pr[:, 0:1], -1.0, A.is_lt, A.mult).then_inc(e3[0], 1)
+    V.tensor_scalar(T.I16[:], T.ni[:], T.pf[:, 0:1], None, A.is_equal).then_inc(e3[0], 1)
+    V.tensor_scalar(T.T0[:], T.ni[:], T.pf[:, 0:1], 2.0, A.is_gt, A.mult).then_inc(e3[0], 1)
+    on(V, e3)
+    on(V, e0)
+    e4 = new(2)
+    V.tensor_tensor(T.MC[:], T.MC0[:], T.MB[:], A.mult).then_inc(e4[0], 1)
+    V.tensor_tensor(T.T2[:], T.T0[:], T.I16[:], A.add).then_inc(e4[0], 1)
+
+    V.wait_ge(T.sem.s_li, 32)
+    V.wait_ge(T.sem.ln_in, ln_all)
+    e5 = new(4)
+    for k in range(4):
+        ph = 2 * (k % 2) + k // 2
+        V.tensor_copy(T.Lf[:, 8 + k:8 + 8 * nr:8], T.Li[:, ph:4 * nr:4]).then_inc(e5[0], 1)
+    on(V, e5)
+    cb, n = 8 * (lo + 1), 8 * nw - 4
+    top = 8 * (hi + 2)
+    e6 = new(1)
+    V.tensor_tensor_scan(T.S[:, 0:top], T.ones[:, 0:top], T.Lf[:, 0:top], 0.0, A.mult, A.add).then_inc(e6[0], 1)
+    on(P, e3)
+    on(P, e4)
+    on(P, e5)
+    P.matmul(T.psE[:, 0:n], T.MC[:], T.Lf[:, cb:cb + n], True, False)
+    on(P, e6)
+    P.matmul(T.psE[:, 0:n], T.MB[:], T.S[:, cb:cb + n], False, False)
+    P.matmul(T.psE[:, 0:n], T.MA[:], T.S[:, cb + 4:cb + 4 + n], False, False)
+    e7 = new(1)
+    P.matmul(T.psE[:, 0:n], T.MD[:], T.S[:, cb - 4:cb - 4 + n], False, True).then_inc(e7[0], 1)
+    on(V, e7)
+    e8 = new(2)
+    base = 128.0 * s - 128.0
+    V.tensor_scalar(T.Abf[:, 0:n], T.psE[:, 0:n], base + 0.46875, 128.0, A.subtract, A.max).then_inc(e8[0], 1)
+    V.tensor_scalar(T.Ff[:, 0:n], T.psE[:, 0:n], base, 128.0, A.subtract, A.max).then_inc(e8[0], 1)
+    on(V, e8)
+    e9 = new(1)
+    V.tensor_tensor(T.Bf[:, 0:n], T.Ff[:, 0:n], T.Abf[:, 0:n], A.subtract).then_inc(e9[0], 1)
+
+    nt = 4 * nw
+    cols = [8 * (t // 4) + t % 4 for t in range(nt)]
+    by_s = [t for t in range(nt) if t % 2 == 1 and t < nt - 2]
+    tile = [new(2) for t in range(nt)]
+
+    def one_hot(t):
+        o, a = T.OA[:, 128 * t:128 * t + 128], T.Abf[:, cols[t]:cols[t] + 1]
+        if t in by_s:
+            V.tensor_scalar(o, T.iq[:], a, -0.5, A.is_equal, A.mult).then_inc(tile[t][0], 1)
+        else:
+            V.tensor_scalar(o, T.iq[:], a, None, A.is_equal).then_inc(tile[t][0], 1)
+
+    ahead = 3
+    for t in range(ahead):
+        one_hot(t)
+    on(V, e9)
+    on(S, e2)
+    on(S, e9)
+    for t in range(nt):
+        o, b = T.OB[:, 128 * t:128 * t + 128], T.Bf[:, cols[t]:cols[t] + 1]
+        if t in by_s:
+            S.activation(o, T.im[:], F.Sign, bias=b, scale=-1.0).then_inc(tile[t][0], 1)
+        else:
+            V.tensor_scalar(o, T.im[:], b, 0.5, A.is_ge, A.subtract).then_inc(tile[t][0], 1)
+        if t + ahead < nt:
+            one_hot(t + ahead)
+    e10 = new(1)
+    for t in range(nt):
+        on(P, tile[t])
+        m = P.matmul(T.psH[:, 0:128], T.OA[:, 128 * t:128 * t + 128], T.OB[:, 128 * t:128 * t + 128], t == 0, t == nt - 1)
+        if t == nt - 1:
+            m.then_inc(e10[0], 1)
+    on(V, e10)
+    e11 = new(2)
+    V.tensor_copy(T.Hs[:], T.psH[:, 0:128]).then_inc(e11[0], 1)
+    V.tensor_scalar(T.H15[:], T.oneh[:], T.psH[:, 15:16], None, A.mult).then_inc(e11[0], 1)
+    on(P, e11)
+    P.matmul(T.psC[:, 0:128], T.Hs[:], T.I16[:], True, False)
+    e12 = new(1)
+    P.matmul(T.psC[:, 0:128], T.H15[:], T.T2[:], False, True).then_inc(e12[0], 1)
+    on(V, e12)
+    e13 = new(1)
+    V.tensor_copy(T.off[:], T.psC[:, 0:128]).then_inc(e13[0], 1)
+
+    W = nw * J + 4
+    for q in (V, S):
+        on(q, e13)
+        q.wait_ge(T.sem.s_w, 16)
+        q.wait_ge(T.sem.x_in, x_all)
+    on(S, e0)
+    for k in (0, 1):
+        e = new(1)
+        V.tensor_copy(T.yb[:, 512 * k:512 * k + 512], T.win[:, 0:W].indirect(T.off[:, 32 * k:32 * k + 32])).then_inc(e[0], 1)
+        on(g.sync, e)
+        g.sync.dma_start(T.y[:, 512 * k:512 * k + 512], T.yb[:, 512 * k:512 * k + 512]).then_inc(T.sem.s_yv, 16)
+        k += 2
+        e = new(1)
+        S.activation(T.yb[:, 512 * k:512 * k + 512], T.win[:, 0:W].indirect(T.off[:, 32 * k:32 * k + 32]), F.Copy,
+                     bias=-0.0).then_inc(e[0], 1)
+        on(S, e)
+        g.scalar.dma_start(T.y[:, 512 * k:512 * k + 512], T.yb[:, 512 * k:512 * k + 512]).then_inc(T.sem.s_ys, 16)
+    g.sync.wait_ge(T.sem.s_yv, 32)
+    g.scalar.wait_ge(T.sem.s_ys, 32)
+    g.wait_ge(T.sem.ls, sent)

@@ -4,33 +4,38 @@ from concourse.mybir import AluOpType as A, ActivationFunctionType as F
 N, J, Q = 6, 512, 2048
 SIM = 256
 WZ = 3 * J + 4
+H = J // 2
+FIRST = 384
+SW = 64
 
 SCRATCH = {
-    "lnd": ("dram", [2, 128, 2], "int32"),
-    "xd": ("dram", [2, 128, 256], "float32"),
-    "lnh": ("dram", [128, 2], "int32"),
-    "xh": ("dram", [128, 256], "float32"),
-    "Li": ("sbuf", [128, 4 * N], "int32"),
+    "lnd": ("dram", [128, 4], "int32"),
+    "xd": ("dram", [2, 128, H], "float32"),
+    "lnh": ("dram", [128, 4], "int32"),
+    "xh": ("dram", [128, H], "float32"),
+    "Li": ("sbuf", [128, 8 * (N + 1)], "int32"),
     "win": ("sbuf", [128, WZ], "float32"),
     "ni": ("sbuf", [128, 128], "int32"), "pi": ("sbuf", [128, 4], "int32"),
-    "bi": ("sbuf", [128, 128], "int32"), "ri": ("sbuf", [128, 128], "int32"),
+    "bi": ("sbuf", [128, 128], "int32"), "ri": ("sbuf", [128, 128], "int32"), "mi": ("sbuf", [128, 64], "int32"),
     "pbi": ("sbuf", [128, 4], "int32"), "pri": ("sbuf", [128, 4], "int32"),
     "pb": ("sbuf", [128, 4], "float32"), "pr": ("sbuf", [128, 4], "float32"), "pf": ("sbuf", [128, 4], "float32"),
-    "MA": ("sbuf", [128, 128], "float32"), "MB": ("sbuf", [128, 128], "float32"), "MD": ("sbuf", [128, 128], "float32"),
-    "MC0": ("sbuf", [128, 128], "float32"), "MC": ("sbuf", [128, 128], "float32"),
+    "MA": ("sbuf", [128, 128], "float16"), "MB": ("sbuf", [128, 128], "float16"), "MD": ("sbuf", [128, 128], "float16"),
+    "MC0": ("sbuf", [128, 128], "float32"), "MB4": ("sbuf", [128, 128], "float32"), "MC": ("sbuf", [128, 128], "float32"),
     "I16": ("sbuf", [128, 128], "float16"), "T0": ("sbuf", [128, 128], "float16"), "T2": ("sbuf", [128, 128], "float16"),
-    "iq": ("sbuf", [128, 128], "bfloat16"), "im": ("sbuf", [128, 128], "bfloat16"),
+    "iq": ("sbuf", [128, 128], "bfloat16"), "im": ("sbuf", [128, 64], "float32"),
     "oneh": ("sbuf", [128, 128], "float16"), "ones": ("sbuf", [128, 56], "float32"),
     "Lf": ("sbuf", [128, 56], "float32"), "S": ("sbuf", [128, 56], "float32"),
-    "Abf": ("sbuf", [128, 24], "bfloat16"), "Ff": ("sbuf", [128, 24], "float32"), "Bf": ("sbuf", [128, 24], "float32"),
-    "OA": ("sbuf", [128, 12 * 128], "bfloat16"), "OB": ("sbuf", [128, 12 * 128], "bfloat16"),
+    "Sh": ("sbuf", [128, 56], "float16"), "Sl": ("sbuf", [128, 56], "float16"),
+    "Abf": ("sbuf", [128, 24], "bfloat16"), "Bf": ("sbuf", [128, 24], "float32"),
+    "OA": ("sbuf", [128, 12 * 128], "bfloat16"), "OB": ("sbuf", [128, 12 * SW], "bfloat16"),
     "Hs": ("sbuf", [128, 128], "float16"), "H15": ("sbuf", [128, 128], "float16"),
     "off": ("sbuf", [128, 128], "uint16"),
     "yb": ("sbuf", [128, Q], "float32"),
-    "psE": ("psum", [128, 512], "float32"), "psH": ("psum", [128, 512], "float32"), "psC": ("psum", [128, 512], "float32"),
+    "psE": ("psum", [128, 512], "float32"), "psH": ("psum", [128, 512], "float32"),
+    "psC": ("psum", [128, 512], "float32"), "psD": ("psum", [128, 512], "float32"),
 }
 EV = ["e%d" % i for i in range(48)]
-SEMAPHORES = ["s_lnd", "s_xd", "s_li", "s_w", "s_yv", "s_ys", "ln_in", "x_in", "hl", "hx", "ls"] + EV
+SEMAPHORES = ["s_lnd", "s_x0", "s_x1", "s_li", "s_w", "s_y", "ln_in", "x_in", "hl", "hx", "ls", "lx"] + EV
 
 
 def _bits(mask):
@@ -53,20 +58,29 @@ def _slot(r, d):
     return (r - max(d - 1, 0)) * J
 
 
-def _helpers(r, T, topo):
+def _plan(r, T, topo):
     me = T.cores[r]
-    far = [d for d in _lists_to(r) if not topo.may_write(me, T.cores[d])]
-    if not far:
-        return {}
-    chip = [c for c in range(SIM) if c != me and topo.host(c) == topo.host(me) and topo.chip(c) == topo.chip(me)
-            and all(topo.may_write(c, T.cores[d]) for d in far)]
-    own = [c for c in chip if topo.die(c) == topo.die(me)]
-    oth = [c for c in chip if topo.die(c) != topo.die(me)]
-    plan = {}
-    for k, d in enumerate(far):
-        plan[(d, 0)] = own[k]
-        plan[(d, 1)] = oth[k]
-    return plan
+    reach = [topo.may_write(me, c) for c in T.cores]
+    chip = [c for c in range(SIM) if c != me and topo.host(c) == topo.host(me) and topo.chip(c) == topo.chip(me)]
+    out = T.cores[reach.index(False)]
+    gate = [[c for c in chip if topo.may_write(c, out) and (topo.die(c) == topo.die(me)) == own] for own in (True, False)]
+    rest = [[c for c in chip if not topo.may_write(c, out) and (topo.die(c) == topo.die(me)) == own] for own in (True, False)]
+    job = {c: [None, None] for c in chip}
+    gates, rests, direct = [list(a) for a in gate], [list(a) for a in rest], None
+    for d in _x_to(r):
+        if not reach[d]:
+            job[gates[0].pop(0)][1] = (d, 0)
+            job[gates[1].pop(0)][1] = (d, 1)
+        else:
+            job[rests[1].pop(0)][1] = (d, 1)
+            if direct is None:
+                direct = d
+            else:
+                job[rests[0].pop(0)][1] = (d, 0)
+    for d in sorted(_lists_to(r), key=lambda d: reach[d]):
+        free = [c for c in (chip if reach[d] else gate[0] + gate[1]) if job[c][0] is None]
+        job[min(free, key=lambda c: (job[c][1] is None, job[c][1] is not None and job[c][1][0] != d))][0] = d
+    return job, direct
 
 
 def _xfer(topo, src_core, cores, engines, sem, src, dsts):
@@ -77,39 +91,41 @@ def _xfer(topo, src_core, cores, engines, sem, src, dsts):
     return RemoteDMATransfer(dst_ids=ids, dma_engine_mask=_mask(engines), remote_sem=sem, srcs=[src], dsts=dsts, alu_op=0)
 
 
-def _helper_program(g, core, T, topo, r, d, half):
-    dst = T.cores[d]
-    eng = _bits(topo.mask(core, dst))
+def _helper_program(g, core, T, topo, r, to_l, to_x):
     n = 0
-    g.wait_ge(T.sem.hl, 1)
-    g.remote_dma_fused([_xfer(topo, core, [dst], eng, T.sem.ln_in, T.lnh[:],
-                              [T.Li[:, 4 * r + 2 * half:4 * r + 2 * half + 2]])], local_sem=T.sem.ls)
-    n += len(eng)
-    if d in _x_to(r):
-        g.wait_ge(T.sem.hx, len(_bits(topo.mask(T.cores[r], core))) // 2)
-        o = _slot(r, d) + 256 * half
-        g.remote_dma_fused([_xfer(topo, core, [dst], eng, T.sem.x_in, T.xh[:], [T.win[:, o:o + 256]])],
+    if to_l is not None:
+        dst = T.cores[to_l]
+        eng = _bits(topo.mask(core, dst))
+        g.wait_ge(T.sem.hl, 2)
+        g.remote_dma_fused([_xfer(topo, core, [dst], eng, T.sem.ln_in, T.lnh[:], [T.Li[:, 8 * r + 8:8 * r + 12]])],
                            local_sem=T.sem.ls)
         n += len(eng)
-    g.wait_ge(T.sem.ls, n)
+    if to_x is not None:
+        d, half = to_x
+        dst = T.cores[d]
+        eng = _bits(topo.mask(core, dst))
+        o = _slot(r, d) + H * half
+        g.wait_ge(T.sem.hx, len(_bits(topo.mask(T.cores[r], core))))
+        g.remote_dma_fused([_xfer(topo, core, [dst], eng, T.sem.x_in, T.xh[:], [T.win[:, o:o + H]])], local_sem=T.sem.ls)
+        n += len(eng)
+    if n:
+        g.wait_ge(T.sem.ls, n)
 
 
 def rank_program(g, core, T, topo):
     s = T.rank_of(core)
     if s is None:
         for r in range(N):
-            for (d, half), c in _helpers(r, T, topo).items():
-                if c == core:
-                    _helper_program(g, core, T, topo, r, d, half)
+            if topo.host(core) == topo.host(T.cores[r]) and topo.chip(core) == topo.chip(T.cores[r]):
+                job = _plan(r, T, topo)[0]
+                _helper_program(g, core, T, topo, r, job[core][0], job[core][1])
         return
 
-    plan = _helpers(s, T, topo)
-    far_x = [d for d in _x_to(s) if (d, 0) in plan]
-    near_x = [d for d in _x_to(s) if (d, 0) not in plan]
-    far_l = [d for d in _lists_to(s) if (d, 0) in plan]
-    near_l = [d for d in _lists_to(s) if (d, 0) not in plan]
+    job, direct = _plan(s, T, topo)
+    by_l = [c for c in job if job[c][0] is not None]
+    by_x = [[c for c in job if job[c][1] is not None and job[c][1][1] == half] for half in (0, 1)]
     lo, hi = max(s - 1, 0), min(s + 1, N - 1)
-    nw, nr = hi - lo + 1, hi + 1
+    nw = hi - lo + 1
     own = _slot(s, s)
     V, S, P = g.vector, g.scalar, g.tensor
     free = [0]
@@ -121,188 +137,168 @@ def rank_program(g, core, T, topo):
     def on(q, e):
         q.wait_ge(e[0], e[1])
 
-    if far_l:
-        g.scalar.dma_start(T.lnd[:], T.ln[:]).then_inc(T.sem.s_lnd, 16)
-    if far_x:
-        g.sync.dma_start(T.xd[0], T.x[:, 0:256]).then_inc(T.sem.s_xd, 16)
-        g.scalar.dma_start(T.xd[1], T.x[:, 256:512]).then_inc(T.sem.s_xd, 16)
-    else:
-        g.sync.dma_start(T.win[:, own:own + J], T.x[:]).then_inc(T.sem.s_w, 16)
-    g.scalar.dma_start(T.Li[:, 4 * s:4 * s + 2], T.ln[0:8, :]).then_inc(T.sem.s_li, 16)
-    g.scalar.dma_start(T.Li[:, 4 * s + 2:4 * s + 4], T.ln[8:16, :]).then_inc(T.sem.s_li, 16)
-    if far_x:
-        g.sync.wait_ge(T.sem.s_xd, 32)
-        g.sync.dma_start(T.win[:, own:own + J], T.x[:]).then_inc(T.sem.s_w, 16)
+    g.scalar.dma_start(T.lnd[:], T.ln[:]).then_inc(T.sem.s_lnd, 16)
+    g.sync.dma_start(T.xd[1], T.x[:, H:J]).then_inc(T.sem.s_x1, 16)
+    g.scalar.dma_start(T.xd[0], T.x[:, 0:H]).then_inc(T.sem.s_x0, 16)
+    g.scalar.dma_start(T.Li[:, 8 * s + 8:8 * s + 12], T.ln[:]).then_inc(T.sem.s_li, 16)
 
     e_io = new(2)
     g.iota(T.ni[:, 0:128], [[1, 128]], 0, 0).then_inc(e_io[0], 1)
     g.iota(T.pi[:, 0:1], [[0, 1]], 0, 1).then_inc(e_io[0], 1)
-    sent = 0
-    if far_l:
-        g.wait_ge(T.sem.s_lnd, 16)
-        eng = _bits(topo.mask(core, plan[(far_l[0], 0)]))
-        tr = []
-        for half in (0, 1):
-            cs = [plan[(d, half)] for d in far_l]
-            tr.append(_xfer(topo, core, cs, [eng[1 - half]], T.sem.hl, T.lnd[half], [T.lnh[:]] * len(cs)))
-        g.remote_dma_fused(tr, local_sem=T.sem.ls)
-        sent += 2
-    if far_x:
-        g.wait_ge(T.sem.s_xd, 32)
-        eng = _bits(topo.mask(core, plan[(far_x[0], 0)]))
-        tr = []
-        for half in (0, 1):
-            cs = [plan[(d, half)] for d in far_x]
-            tr.append(_xfer(topo, core, cs, eng[1 - half::2], T.sem.hx, T.xd[half], [T.xh[:]] * len(cs)))
-        g.remote_dma_fused(tr, local_sem=T.sem.ls)
+    g.wait_ge(T.sem.s_lnd, 16)
+    eng = _bits(topo.mask(core, by_l[0]))[0:2]
+    g.remote_dma_fused([_xfer(topo, core, by_l, eng, T.sem.hl, T.lnd[:], [T.lnh[:]] * len(by_l))], local_sem=T.sem.ls)
+    sent, sent_x = len(eng), 0
+    for half in (1, 0):
+        g.wait_ge(T.sem["s_x%d" % half], 16)
+        if by_x[half]:
+            eng = _bits(topo.mask(core, by_x[half][0]))
+            g.remote_dma_fused([_xfer(topo, core, by_x[half], eng, T.sem.hx, T.xd[half], [T.xh[:]] * len(by_x[half]))],
+                               local_sem=T.sem.lx)
+            sent_x += len(eng)
+    if direct is not None:
+        dst, o = T.cores[direct], _slot(s, direct)
+        eng = _bits(topo.mask(core, dst))
+        g.remote_dma_fused([_xfer(topo, core, [dst], eng, T.sem.x_in, T.xd[0], [T.win[:, o:o + H]])], local_sem=T.sem.ls)
         sent += len(eng)
-    if near_l:
-        g.wait_ge(T.sem.s_li, 32)
-        eng = _bits(topo.mask(core, T.cores[near_l[0]]))
-        ap = T.Li[:, 4 * s:4 * s + 4]
-        g.remote_dma_fused([_xfer(topo, core, [T.cores[d] for d in near_l], eng, T.sem.ln_in, ap, [ap] * len(near_l))],
-                           local_sem=T.sem.ls)
-        sent += len(eng)
-    if near_x:
-        g.wait_ge(T.sem.s_w, 16)
-        eng = _bits(topo.mask(core, T.cores[near_x[0]]))
-        g.remote_dma_fused([_xfer(topo, core, [T.cores[d] for d in near_x], eng, T.sem.x_in, T.win[:, own:own + J],
-                                  [T.win[:, _slot(s, d):_slot(s, d) + J] for d in near_x])], local_sem=T.sem.ls)
-        sent += len(eng)
+
+    g.sync.wait_ge(T.sem.lx, sent_x)
+    g.sync.dma_start(T.win[:, own:own + J], T.x[:]).then_inc(T.sem.s_w, 16)
 
     ln_all = x_all = 0
     for r in range(N):
-        if r == s or s not in _lists_to(r):
-            continue
-        p = _helpers(r, T, topo)
-        from_cores = [p[(s, 0)], p[(s, 1)]] if (s, 0) in p else [T.cores[r]]
-        cnt = sum(len(_bits(topo.mask(c, core))) for c in from_cores)
-        ln_all += cnt
-        if s in _x_to(r):
-            x_all += cnt
+        if r != s:
+            pj, pd = _plan(r, T, topo)
+            for c in pj:
+                n = len(_bits(topo.mask(c, core)))
+                if pj[c][0] == s:
+                    ln_all += n
+                if pj[c][1] is not None and pj[c][1][0] == s:
+                    x_all += n
+            if pd == s:
+                x_all += len(_bits(topo.mask(T.cores[r], core)))
 
-    e0 = new(3)
-    V.memset(T.Lf[:], 0.0).then_inc(e0[0], 1)
+    base = 128.0 * s - 128.0
+    e0 = new(7)
     V.memset(T.ones[:], 1.0).then_inc(e0[0], 1)
     V.memset(T.win[:, nw * J:nw * J + 4], 0.0).then_inc(e0[0], 1)
+    V.memset(T.Li[:, 0:4], 0).then_inc(e0[0], 1)
+    for k in range(4, 8):
+        V.memset(T.Li[:, k:8 * (hi + 2):8], 0).then_inc(e0[0], 1)
     on(V, e_io)
     e1 = new(6)
-    V.tensor_scalar(T.bi[:], T.ni[:], 15, None, A.bitwise_and).then_inc(e1[0], 1)
-    V.tensor_scalar(T.ri[:], T.ni[:], 4, None, A.arith_shift_right).then_inc(e1[0], 1)
-    V.tensor_scalar(T.pbi[:, 0:1], T.pi[:, 0:1], 15, None, A.bitwise_and).then_inc(e1[0], 1)
-    V.tensor_scalar(T.pri[:, 0:1], T.pi[:, 0:1], 4, None, A.arith_shift_right).then_inc(e1[0], 1)
-    V.tensor_scalar(T.iq[:], T.ni[:], 128.0, None, A.add).then_inc(e1[0], 1)
-    V.tensor_scalar(T.oneh[:], T.ni[:], 0.0, 1.0, A.mult, A.add).then_inc(e1[0], 1)
+    V.tensor_scalar(T.bi[:], T.ni[:], 7, None, A.bitwise_and).then_inc(e1[0], 1)
+    V.tensor_scalar(T.ri[:], T.ni[:], 3, None, A.arith_shift_right).then_inc(e1[0], 1)
+    V.tensor_scalar(T.mi[:], T.ni[:, 0:SW], 15, None, A.bitwise_and).then_inc(e1[0], 1)
+    V.tensor_scalar(T.pbi[:, 0:1], T.pi[:, 0:1], 7, None, A.bitwise_and).then_inc(e1[0], 1)
+    V.tensor_scalar(T.pri[:, 0:1], T.pi[:, 0:1], 3, None, A.arith_shift_right).then_inc(e1[0], 1)
+    V.tensor_copy(T.pf[:, 0:1], T.pi[:, 0:1]).then_inc(e1[0], 1)
     on(V, e1)
-    e2 = new(4)
+    e2 = new(5)
     V.tensor_copy(T.pb[:, 0:1], T.pbi[:, 0:1]).then_inc(e2[0], 1)
     V.tensor_copy(T.pr[:, 0:1], T.pri[:, 0:1]).then_inc(e2[0], 1)
-    V.tensor_copy(T.pf[:, 0:1], T.pi[:, 0:1]).then_inc(e2[0], 1)
-    V.tensor_scalar(T.im[:], T.bi[:], 1.0 / 16, 1.0 / 32, A.mult, A.add).then_inc(e2[0], 1)
+    V.tensor_scalar(T.im[:], T.mi[:], 1.0 / 16, 1.0 / 32 + base, A.mult, A.add).then_inc(e2[0], 1)
+    V.tensor_scalar(T.iq[:], T.ni[:], 128.0, None, A.add).then_inc(e2[0], 1)
+    V.tensor_scalar(T.oneh[:], T.ni[:], 0.0, 1.0, A.mult, A.add).then_inc(e2[0], 1)
     on(V, e2)
-    e3 = new(6)
+    e3 = new(7)
     V.tensor_scalar(T.MA[:], T.bi[:], T.pb[:, 0:1], 1.0 / 16, A.is_gt, A.mult).then_inc(e3[0], 1)
     V.tensor_scalar(T.MB[:], T.bi[:], T.pb[:, 0:1], 1.0 / 16, A.is_equal, A.mult).then_inc(e3[0], 1)
     V.tensor_scalar(T.MD[:], T.bi[:], T.pb[:, 0:1], 1.0 / 16, A.is_lt, A.mult).then_inc(e3[0], 1)
-    V.tensor_scalar(T.MC0[:], T.ri[:], T.pr[:, 0:1], -1.0, A.is_lt, A.mult).then_inc(e3[0], 1)
+    V.tensor_scalar(T.MC0[:], T.ri[:], T.pr[:, 0:1], -1.0 / 16, A.is_lt, A.mult).then_inc(e3[0], 1)
+    V.tensor_scalar(T.MB4[:], T.bi[:], T.pb[:, 0:1], None, A.is_equal).then_inc(e3[0], 1)
     V.tensor_scalar(T.I16[:], T.ni[:], T.pf[:, 0:1], None, A.is_equal).then_inc(e3[0], 1)
     V.tensor_scalar(T.T0[:], T.ni[:], T.pf[:, 0:1], 2.0, A.is_gt, A.mult).then_inc(e3[0], 1)
     on(V, e3)
-    on(V, e0)
     e4 = new(2)
-    V.tensor_tensor(T.MC[:], T.MC0[:], T.MB[:], A.mult).then_inc(e4[0], 1)
+    V.tensor_tensor(T.MC[:], T.MC0[:], T.MB4[:], A.mult).then_inc(e4[0], 1)
     V.tensor_tensor(T.T2[:], T.T0[:], T.I16[:], A.add).then_inc(e4[0], 1)
 
-    V.wait_ge(T.sem.s_li, 32)
-    V.wait_ge(T.sem.ln_in, ln_all)
-    e5 = new(4)
-    for k in range(4):
-        ph = 2 * (k % 2) + k // 2
-        V.tensor_copy(T.Lf[:, 8 + k:8 + 8 * nr:8], T.Li[:, ph:4 * nr:4]).then_inc(e5[0], 1)
-    on(V, e5)
-    cb, n = 8 * (lo + 1), 8 * nw - 4
     top = 8 * (hi + 2)
-    e6 = new(1)
-    V.tensor_tensor_scan(T.S[:, 0:top], T.ones[:, 0:top], T.Lf[:, 0:top], 0.0, A.mult, A.add).then_inc(e6[0], 1)
+    cb, n = 8 * (lo + 1), 8 * nw - 4
     on(P, e3)
     on(P, e4)
+    on(S, e0)
+    on(S, e2)
+    on(V, e0)
+    V.wait_ge(T.sem.s_li, 16)
+    V.wait_ge(T.sem.ln_in, ln_all)
+    e5, e6, e7, e8 = new(1), new(1), new(1), new(1)
+    V.tensor_copy(T.Lf[:, 0:top], T.Li[:, 0:top]).then_inc(e5[0], 1)
+    on(V, e5)
+    V.tensor_tensor_scan(T.Sh[:, 0:top], T.ones[:, 0:top], T.Lf[:, 0:top], 0.0, A.mult, A.add).then_inc(e6[0], 1)
+    V.tensor_tensor_scan(T.S[:, 0:top], T.ones[:, 0:top], T.Lf[:, 0:top], 0.0, A.mult, A.add).then_inc(e7[0], 1)
+    on(V, e6)
+    on(V, e7)
+    V.tensor_tensor(T.Sl[:, 0:top], T.S[:, 0:top], T.Sh[:, 0:top], A.subtract).then_inc(e8[0], 1)
     on(P, e5)
     P.matmul(T.psE[:, 0:n], T.MC[:], T.Lf[:, cb:cb + n], True, False)
-    on(P, e6)
-    P.matmul(T.psE[:, 0:n], T.MB[:], T.S[:, cb:cb + n], False, False)
-    P.matmul(T.psE[:, 0:n], T.MA[:], T.S[:, cb + 4:cb + 4 + n], False, False)
-    e7 = new(1)
-    P.matmul(T.psE[:, 0:n], T.MD[:], T.S[:, cb - 4:cb - 4 + n], False, True).then_inc(e7[0], 1)
-    on(V, e7)
-    e8 = new(2)
-    base = 128.0 * s - 128.0
-    V.tensor_scalar(T.Abf[:, 0:n], T.psE[:, 0:n], base + 0.46875, 128.0, A.subtract, A.max).then_inc(e8[0], 1)
-    V.tensor_scalar(T.Ff[:, 0:n], T.psE[:, 0:n], base, 128.0, A.subtract, A.max).then_inc(e8[0], 1)
-    on(V, e8)
-    e9 = new(1)
-    V.tensor_tensor(T.Bf[:, 0:n], T.Ff[:, 0:n], T.Abf[:, 0:n], A.subtract).then_inc(e9[0], 1)
+    for src, e in ((T.Sh, e6), (T.Sl, e8)):
+        on(P, e)
+        P.matmul(T.psE[:, 0:n], T.MB[:], src[:, cb:cb + n], False, False)
+        P.matmul(T.psE[:, 0:n], T.MA[:], src[:, cb + 4:cb + 4 + n], False, False)
+        m = P.matmul(T.psE[:, 0:n], T.MD[:], src[:, cb - 4:cb - 4 + n], False, e is e8)
+    e9, e10, e11 = new(1), new(1), new(1)
+    m.then_inc(e9[0], 1)
+    on(V, e9)
+    V.tensor_scalar(T.Abf[:, 0:n], T.psE[:, 0:n], base + 0.46875, 128.0, A.subtract, A.max).then_inc(e10[0], 1)
+    on(V, e10)
+    V.tensor_tensor(T.Bf[:, 0:n], T.psE[:, 0:n], T.Abf[:, 0:n], A.subtract).then_inc(e11[0], 1)
 
     nt = 4 * nw
     cols = [8 * (t // 4) + t % 4 for t in range(nt)]
-    by_s = [t for t in range(nt) if t % 2 == 1 and t < nt - 2]
+    by_v = (0, nt // 2, nt - 1)
     tile = [new(2) for t in range(nt)]
-
-    def one_hot(t):
-        o, a = T.OA[:, 128 * t:128 * t + 128], T.Abf[:, cols[t]:cols[t] + 1]
-        if t in by_s:
-            V.tensor_scalar(o, T.iq[:], a, -0.5, A.is_equal, A.mult).then_inc(tile[t][0], 1)
-        else:
-            V.tensor_scalar(o, T.iq[:], a, None, A.is_equal).then_inc(tile[t][0], 1)
-
-    ahead = 3
-    for t in range(ahead):
-        one_hot(t)
-    on(V, e9)
-    on(S, e2)
-    on(S, e9)
+    oa = [T.OA[:, 128 * t:128 * t + 128] for t in range(nt)]
+    ob = [T.OB[:, SW * t:SW * t + SW] for t in range(nt)]
     for t in range(nt):
-        o, b = T.OB[:, 128 * t:128 * t + 128], T.Bf[:, cols[t]:cols[t] + 1]
-        if t in by_s:
-            S.activation(o, T.im[:], F.Sign, bias=b, scale=-1.0).then_inc(tile[t][0], 1)
+        a, b = T.Abf[:, cols[t]:cols[t] + 1], T.Bf[:, cols[t]:cols[t] + 1]
+        if t in by_v:
+            V.tensor_scalar(oa[t], T.iq[:], a, None, A.is_equal).then_inc(tile[t][0], 1)
+            if t == 0:
+                on(V, e11)
+            V.tensor_scalar(ob[t], T.im[:], b, 0.5, A.is_ge, A.subtract).then_inc(tile[t][0], 1)
         else:
-            V.tensor_scalar(o, T.im[:], b, 0.5, A.is_ge, A.subtract).then_inc(tile[t][0], 1)
-        if t + ahead < nt:
-            one_hot(t + ahead)
-    e10 = new(1)
+            V.tensor_scalar(oa[t], T.iq[:], a, -0.5, A.is_equal, A.mult).then_inc(tile[t][0], 1)
+    on(S, e11)
+    for t in range(nt):
+        if t not in by_v:
+            S.activation(ob[t], T.im[:], F.Sign, bias=T.Bf[:, cols[t]:cols[t] + 1], scale=-1.0).then_inc(tile[t][0], 1)
     for t in range(nt):
         on(P, tile[t])
-        m = P.matmul(T.psH[:, 0:128], T.OA[:, 128 * t:128 * t + 128], T.OB[:, 128 * t:128 * t + 128], t == 0, t == nt - 1)
-        if t == nt - 1:
-            m.then_inc(e10[0], 1)
-    on(V, e10)
-    e11 = new(2)
-    V.tensor_copy(T.Hs[:], T.psH[:, 0:128]).then_inc(e11[0], 1)
-    V.tensor_scalar(T.H15[:], T.oneh[:], T.psH[:, 15:16], None, A.mult).then_inc(e11[0], 1)
-    on(P, e11)
-    P.matmul(T.psC[:, 0:128], T.Hs[:], T.I16[:], True, False)
-    e12 = new(1)
-    P.matmul(T.psC[:, 0:128], T.H15[:], T.T2[:], False, True).then_inc(e12[0], 1)
+        m = P.matmul(T.psH[:, 0:SW], oa[t], ob[t], t == 0, t == nt - 1)
+    e12, e13, e14 = new(1), new(1), new(128 // SW)
+    m.then_inc(e12[0], 1)
     on(V, e12)
-    e13 = new(1)
-    V.tensor_copy(T.off[:], T.psC[:, 0:128]).then_inc(e13[0], 1)
+    V.tensor_scalar(T.H15[:], T.oneh[:], T.psH[:, 15:16], None, A.mult).then_inc(e13[0], 1)
+    for k in range(0, 128, SW):
+        V.tensor_copy(T.Hs[:, k:k + SW], T.psH[:, 0:SW]).then_inc(e14[0], 1)
+    c1 = 2 * FIRST // 16
+    parts = ((T.psC, 0, c1), (T.psD, c1, 128))
+    on(P, e13)
+    for ps, a, b in parts:
+        P.matmul(ps[:, 0:b - a], T.H15[:], T.T2[:, a:b], True, False)
+    on(P, e14)
+    ready = []
+    for ps, a, b in parts:
+        e, f = new(1), new(1)
+        P.matmul(ps[:, 0:b - a], T.Hs[:], T.I16[:, a:b], False, True).then_inc(e[0], 1)
+        on(V, e)
+        V.tensor_copy(T.off[:, a:b], ps[:, 0:b - a]).then_inc(f[0], 1)
+        ready.append(f)
 
     W = nw * J + 4
-    for q in (V, S):
-        on(q, e13)
-        q.wait_ge(T.sem.s_w, 16)
-        q.wait_ge(T.sem.x_in, x_all)
-    on(S, e0)
-    for k in (0, 1):
-        e = new(1)
-        V.tensor_copy(T.yb[:, 512 * k:512 * k + 512], T.win[:, 0:W].indirect(T.off[:, 32 * k:32 * k + 32])).then_inc(e[0], 1)
-        on(g.sync, e)
-        g.sync.dma_start(T.y[:, 512 * k:512 * k + 512], T.yb[:, 512 * k:512 * k + 512]).then_inc(T.sem.s_yv, 16)
-        k += 2
-        e = new(1)
-        S.activation(T.yb[:, 512 * k:512 * k + 512], T.win[:, 0:W].indirect(T.off[:, 32 * k:32 * k + 32]), F.Copy,
+    for k, (o, w) in enumerate(((0, FIRST), (2 * FIRST, Q // 2 - FIRST))):
+        e = new(2)
+        for q in (V, S):
+            on(q, ready[k])
+            if k == 0:
+                q.wait_ge(T.sem.s_w, 16)
+                q.wait_ge(T.sem.x_in, x_all)
+        V.tensor_copy(T.yb[:, o:o + w], T.win[:, 0:W].indirect(T.off[:, o // 16:(o + w) // 16])).then_inc(e[0], 1)
+        S.activation(T.yb[:, o + w:o + 2 * w], T.win[:, 0:W].indirect(T.off[:, (o + w) // 16:(o + 2 * w) // 16]), F.Copy,
                      bias=-0.0).then_inc(e[0], 1)
-        on(S, e)
-        g.scalar.dma_start(T.y[:, 512 * k:512 * k + 512], T.yb[:, 512 * k:512 * k + 512]).then_inc(T.sem.s_ys, 16)
-    g.sync.wait_ge(T.sem.s_yv, 32)
-    g.scalar.wait_ge(T.sem.s_ys, 32)
+        on(g.sync, e)
+        g.sync.dma_start(T.y[:, o:o + 2 * w], T.yb[:, o:o + 2 * w]).then_inc(T.sem.s_y, 16)
+    g.sync.wait_ge(T.sem.s_y, 32)
     g.wait_ge(T.sem.ls, sent)

from concourse.bass import DstId, RemoteDMATransfer
from concourse.mybir import AluOpType as A, ActivationFunctionType as F

N, J, Q = 6, 512, 2048
SIM = 256
WZ = 3 * J + 4
H = J // 2
FIRST = 384
SW = 64

SCRATCH = {
    "lnd": ("dram", [128, 4], "int32"),
    "xd": ("dram", [2, 128, H], "float32"),
    "lnh": ("dram", [128, 4], "int32"),
    "xh": ("dram", [128, H], "float32"),
    "Li": ("sbuf", [128, 8 * (N + 1)], "int32"),
    "win": ("sbuf", [128, WZ], "float32"),
    "ni": ("sbuf", [128, 128], "int32"), "pi": ("sbuf", [128, 4], "int32"),
    "bi": ("sbuf", [128, 128], "int32"), "ri": ("sbuf", [128, 128], "int32"), "mi": ("sbuf", [128, 64], "int32"),
    "pbi": ("sbuf", [128, 4], "int32"), "pri": ("sbuf", [128, 4], "int32"),
    "pb": ("sbuf", [128, 4], "float32"), "pr": ("sbuf", [128, 4], "float32"), "pf": ("sbuf", [128, 4], "float32"),
    "MA": ("sbuf", [128, 128], "float16"), "MB": ("sbuf", [128, 128], "float16"), "MD": ("sbuf", [128, 128], "float16"),
    "MC0": ("sbuf", [128, 128], "float32"), "MB4": ("sbuf", [128, 128], "float32"), "MC": ("sbuf", [128, 128], "float32"),
    "I16": ("sbuf", [128, 128], "float16"), "T0": ("sbuf", [128, 128], "float16"), "T2": ("sbuf", [128, 128], "float16"),
    "iq": ("sbuf", [128, 128], "bfloat16"), "im": ("sbuf", [128, 64], "float32"),
    "oneh": ("sbuf", [128, 128], "float16"), "ones": ("sbuf", [128, 56], "float32"),
    "Lf": ("sbuf", [128, 56], "float32"), "S": ("sbuf", [128, 56], "float32"),
    "Sh": ("sbuf", [128, 56], "float16"), "Sl": ("sbuf", [128, 56], "float16"),
    "Abf": ("sbuf", [128, 24], "bfloat16"), "Bf": ("sbuf", [128, 24], "float32"),
    "OA": ("sbuf", [128, 12 * 128], "bfloat16"), "OB": ("sbuf", [128, 12 * SW], "bfloat16"),
    "Hs": ("sbuf", [128, 128], "float16"), "H15": ("sbuf", [128, 128], "float16"),
    "off": ("sbuf", [128, 128], "uint16"),
    "yb": ("sbuf", [128, Q], "float32"),
    "psE": ("psum", [128, 512], "float32"), "psH": ("psum", [128, 512], "float32"),
    "psC": ("psum", [128, 512], "float32"), "psD": ("psum", [128, 512], "float32"),
}
EV = ["e%d" % i for i in range(48)]
SEMAPHORES = ["s_lnd", "s_x0", "s_x1", "s_li", "s_w", "s_y", "ln_in", "x_in", "hl", "hx", "ls", "lx"] + EV


def _bits(mask):
    return [e for e in range(16) if (mask >> e) & 1]


def _mask(engines):
    return sum(1 << e for e in engines)


def _lists_to(r):
    return [d for d in range(N) if d != r and d >= r - 1]


def _x_to(r):
    return [d for d in (r - 1, r + 1) if 0 <= d < N]


def _slot(r, d):
    return (r - max(d - 1, 0)) * J


def _plan(r, T, topo):
    me = T.cores[r]
    reach = [topo.may_write(me, c) for c in T.cores]
    chip = [c for c in range(SIM) if c != me and topo.host(c) == topo.host(me) and topo.chip(c) == topo.chip(me)]
    out = T.cores[reach.index(False)]
    gate = [[c for c in chip if topo.may_write(c, out) and (topo.die(c) == topo.die(me)) == own] for own in (True, False)]
    rest = [[c for c in chip if not topo.may_write(c, out) and (topo.die(c) == topo.die(me)) == own] for own in (True, False)]
    job = {c: [None, None] for c in chip}
    gates, rests, direct = [list(a) for a in gate], [list(a) for a in rest], None
    for d in _x_to(r):
        if not reach[d]:
            job[gates[0].pop(0)][1] = (d, 0)
            job[gates[1].pop(0)][1] = (d, 1)
        else:
            job[rests[1].pop(0)][1] = (d, 1)
            if direct is None:
                direct = d
            else:
                job[rests[0].pop(0)][1] = (d, 0)
    for d in sorted(_lists_to(r), key=lambda d: reach[d]):
        free = [c for c in (chip if reach[d] else gate[0] + gate[1]) if job[c][0] is None]
        job[min(free, key=lambda c: (job[c][1] is None, job[c][1] is not None and job[c][1][0] != d))][0] = d
    return job, direct


def _xfer(topo, src_core, cores, engines, sem, src, dsts):
    ids = []
    for c in cores:
        rid, pid = topo.addr(c, src_core)
        ids.append(DstId(rid=rid, pnc=pid))
    return RemoteDMATransfer(dst_ids=ids, dma_engine_mask=_mask(engines), remote_sem=sem, srcs=[src], dsts=dsts, alu_op=0)


def _helper_program(g, core, T, topo, r, to_l, to_x):
    n = 0
    if to_l is not None:
        dst = T.cores[to_l]
        eng = _bits(topo.mask(core, dst))
        g.wait_ge(T.sem.hl, 2)
        g.remote_dma_fused([_xfer(topo, core, [dst], eng, T.sem.ln_in, T.lnh[:], [T.Li[:, 8 * r + 8:8 * r + 12]])],
                           local_sem=T.sem.ls)
        n += len(eng)
    if to_x is not None:
        d, half = to_x
        dst = T.cores[d]
        eng = _bits(topo.mask(core, dst))
        o = _slot(r, d) + H * half
        g.wait_ge(T.sem.hx, len(_bits(topo.mask(T.cores[r], core))))
        g.remote_dma_fused([_xfer(topo, core, [dst], eng, T.sem.x_in, T.xh[:], [T.win[:, o:o + H]])], local_sem=T.sem.ls)
        n += len(eng)
    if n:
        g.wait_ge(T.sem.ls, n)


def rank_program(g, core, T, topo):
    s = T.rank_of(core)
    if s is None:
        for r in range(N):
            if topo.host(core) == topo.host(T.cores[r]) and topo.chip(core) == topo.chip(T.cores[r]):
                job = _plan(r, T, topo)[0]
                _helper_program(g, core, T, topo, r, job[core][0], job[core][1])
        return

    job, direct = _plan(s, T, topo)
    by_l = [c for c in job if job[c][0] is not None]
    by_x = [[c for c in job if job[c][1] is not None and job[c][1][1] == half] for half in (0, 1)]
    lo, hi = max(s - 1, 0), min(s + 1, N - 1)
    nw = hi - lo + 1
    own = _slot(s, s)
    V, S, P = g.vector, g.scalar, g.tensor
    free = [0]

    def new(n):
        free[0] += 1
        return (T.sem[EV[free[0] - 1]], n)

    def on(q, e):
        q.wait_ge(e[0], e[1])

    g.scalar.dma_start(T.lnd[:], T.ln[:]).then_inc(T.sem.s_lnd, 16)
    g.sync.dma_start(T.xd[1], T.x[:, H:J]).then_inc(T.sem.s_x1, 16)
    g.scalar.dma_start(T.xd[0], T.x[:, 0:H]).then_inc(T.sem.s_x0, 16)
    g.scalar.dma_start(T.Li[:, 8 * s + 8:8 * s + 12], T.ln[:]).then_inc(T.sem.s_li, 16)

    e_io = new(2)
    g.iota(T.ni[:, 0:128], [[1, 128]], 0, 0).then_inc(e_io[0], 1)
    g.iota(T.pi[:, 0:1], [[0, 1]], 0, 1).then_inc(e_io[0], 1)
    g.wait_ge(T.sem.s_lnd, 16)
    eng = _bits(topo.mask(core, by_l[0]))[0:2]
    g.remote_dma_fused([_xfer(topo, core, by_l, eng, T.sem.hl, T.lnd[:], [T.lnh[:]] * len(by_l))], local_sem=T.sem.ls)
    sent, sent_x = len(eng), 0
    for half in (1, 0):
        g.wait_ge(T.sem["s_x%d" % half], 16)
        if by_x[half]:
            eng = _bits(topo.mask(core, by_x[half][0]))
            g.remote_dma_fused([_xfer(topo, core, by_x[half], eng, T.sem.hx, T.xd[half], [T.xh[:]] * len(by_x[half]))],
                               local_sem=T.sem.lx)
            sent_x += len(eng)
    if direct is not None:
        dst, o = T.cores[direct], _slot(s, direct)
        eng = _bits(topo.mask(core, dst))
        g.remote_dma_fused([_xfer(topo, core, [dst], eng, T.sem.x_in, T.xd[0], [T.win[:, o:o + H]])], local_sem=T.sem.ls)
        sent += len(eng)

    g.sync.wait_ge(T.sem.lx, sent_x)
    g.sync.dma_start(T.win[:, own:own + J], T.x[:]).then_inc(T.sem.s_w, 16)

    ln_all = x_all = 0
    for r in range(N):
        if r != s:
            pj, pd = _plan(r, T, topo)
            for c in pj:
                n = len(_bits(topo.mask(c, core)))
                if pj[c][0] == s:
                    ln_all += n
                if pj[c][1] is not None and pj[c][1][0] == s:
                    x_all += n
            if pd == s:
                x_all += len(_bits(topo.mask(T.cores[r], core)))

    base = 128.0 * s - 128.0
    e0 = new(7)
    V.memset(T.ones[:], 1.0).then_inc(e0[0], 1)
    V.memset(T.win[:, nw * J:nw * J + 4], 0.0).then_inc(e0[0], 1)
    V.memset(T.Li[:, 0:4], 0).then_inc(e0[0], 1)
    for k in range(4, 8):
        V.memset(T.Li[:, k:8 * (hi + 2):8], 0).then_inc(e0[0], 1)
    on(V, e_io)
    e1 = new(6)
    V.tensor_scalar(T.bi[:], T.ni[:], 7, None, A.bitwise_and).then_inc(e1[0], 1)
    V.tensor_scalar(T.ri[:], T.ni[:], 3, None, A.arith_shift_right).then_inc(e1[0], 1)
    V.tensor_scalar(T.mi[:], T.ni[:, 0:SW], 15, None, A.bitwise_and).then_inc(e1[0], 1)
    V.tensor_scalar(T.pbi[:, 0:1], T.pi[:, 0:1], 7, None, A.bitwise_and).then_inc(e1[0], 1)
    V.tensor_scalar(T.pri[:, 0:1], T.pi[:, 0:1], 3, None, A.arith_shift_right).then_inc(e1[0], 1)
    V.tensor_copy(T.pf[:, 0:1], T.pi[:, 0:1]).then_inc(e1[0], 1)
    on(V, e1)
    e2 = new(5)
    V.tensor_copy(T.pb[:, 0:1], T.pbi[:, 0:1]).then_inc(e2[0], 1)
    V.tensor_copy(T.pr[:, 0:1], T.pri[:, 0:1]).then_inc(e2[0], 1)
    V.tensor_scalar(T.im[:], T.mi[:], 1.0 / 16, 1.0 / 32 + base, A.mult, A.add).then_inc(e2[0], 1)
    V.tensor_scalar(T.iq[:], T.ni[:], 128.0, None, A.add).then_inc(e2[0], 1)
    V.tensor_scalar(T.oneh[:], T.ni[:], 0.0, 1.0, A.mult, A.add).then_inc(e2[0], 1)
    on(V, e2)
    e3 = new(7)
    V.tensor_scalar(T.MA[:], T.bi[:], T.pb[:, 0:1], 1.0 / 16, A.is_gt, A.mult).then_inc(e3[0], 1)
    V.tensor_scalar(T.MB[:], T.bi[:], T.pb[:, 0:1], 1.0 / 16, A.is_equal, A.mult).then_inc(e3[0], 1)
    V.tensor_scalar(T.MD[:], T.bi[:], T.pb[:, 0:1], 1.0 / 16, A.is_lt, A.mult).then_inc(e3[0], 1)
    V.tensor_scalar(T.MC0[:], T.ri[:], T.pr[:, 0:1], -1.0 / 16, A.is_lt, A.mult).then_inc(e3[0], 1)
    V.tensor_scalar(T.MB4[:], T.bi[:], T.pb[:, 0:1], None, A.is_equal).then_inc(e3[0], 1)
    V.tensor_scalar(T.I16[:], T.ni[:], T.pf[:, 0:1], None, A.is_equal).then_inc(e3[0], 1)
    V.tensor_scalar(T.T0[:], T.ni[:], T.pf[:, 0:1], 2.0, A.is_gt, A.mult).then_inc(e3[0], 1)
    on(V, e3)
    e4 = new(2)
    V.tensor_tensor(T.MC[:], T.MC0[:], T.MB4[:], A.mult).then_inc(e4[0], 1)
    V.tensor_tensor(T.T2[:], T.T0[:], T.I16[:], A.add).then_inc(e4[0], 1)

    top = 8 * (hi + 2)
    cb, n = 8 * (lo + 1), 8 * nw - 4
    on(P, e3)
    on(P, e4)
    on(S, e0)
    on(S, e2)
    on(V, e0)
    V.wait_ge(T.sem.s_li, 16)
    V.wait_ge(T.sem.ln_in, ln_all)
    e5, e6, e7, e8 = new(1), new(1), new(1), new(1)
    V.tensor_copy(T.Lf[:, 0:top], T.Li[:, 0:top]).then_inc(e5[0], 1)
    on(V, e5)
    V.tensor_tensor_scan(T.Sh[:, 0:top], T.ones[:, 0:top], T.Lf[:, 0:top], 0.0, A.mult, A.add).then_inc(e6[0], 1)
    V.tensor_tensor_scan(T.S[:, 0:top], T.ones[:, 0:top], T.Lf[:, 0:top], 0.0, A.mult, A.add).then_inc(e7[0], 1)
    on(V, e6)
    on(V, e7)
    V.tensor_tensor(T.Sl[:, 0:top], T.S[:, 0:top], T.Sh[:, 0:top], A.subtract).then_inc(e8[0], 1)
    on(P, e5)
    P.matmul(T.psE[:, 0:n], T.MC[:], T.Lf[:, cb:cb + n], True, False)
    for src, e in ((T.Sh, e6), (T.Sl, e8)):
        on(P, e)
        P.matmul(T.psE[:, 0:n], T.MB[:], src[:, cb:cb + n], False, False)
        P.matmul(T.psE[:, 0:n], T.MA[:], src[:, cb + 4:cb + 4 + n], False, False)
        m = P.matmul(T.psE[:, 0:n], T.MD[:], src[:, cb - 4:cb - 4 + n], False, e is e8)
    e9, e10, e11 = new(1), new(1), new(1)
    m.then_inc(e9[0], 1)
    on(V, e9)
    V.tensor_scalar(T.Abf[:, 0:n], T.psE[:, 0:n], base + 0.46875, 128.0, A.subtract, A.max).then_inc(e10[0], 1)
    on(V, e10)
    V.tensor_tensor(T.Bf[:, 0:n], T.psE[:, 0:n], T.Abf[:, 0:n], A.subtract).then_inc(e11[0], 1)

    nt = 4 * nw
    cols = [8 * (t // 4) + t % 4 for t in range(nt)]
    by_v = (0, nt // 2, nt - 1)
    tile = [new(2) for t in range(nt)]
    oa = [T.OA[:, 128 * t:128 * t + 128] for t in range(nt)]
    ob = [T.OB[:, SW * t:SW * t + SW] for t in range(nt)]
    for t in range(nt):
        a, b = T.Abf[:, cols[t]:cols[t] + 1], T.Bf[:, cols[t]:cols[t] + 1]
        if t in by_v:
            V.tensor_scalar(oa[t], T.iq[:], a, None, A.is_equal).then_inc(tile[t][0], 1)
            if t == 0:
                on(V, e11)
            V.tensor_scalar(ob[t], T.im[:], b, 0.5, A.is_ge, A.subtract).then_inc(tile[t][0], 1)
        else:
            V.tensor_scalar(oa[t], T.iq[:], a, -0.5, A.is_equal, A.mult).then_inc(tile[t][0], 1)
    on(S, e11)
    for t in range(nt):
        if t not in by_v:
            S.activation(ob[t], T.im[:], F.Sign, bias=T.Bf[:, cols[t]:cols[t] + 1], scale=-1.0).then_inc(tile[t][0], 1)
    for t in range(nt):
        on(P, tile[t])
        m = P.matmul(T.psH[:, 0:SW], oa[t], ob[t], t == 0, t == nt - 1)
    e12, e13, e14 = new(1), new(1), new(128 // SW)
    m.then_inc(e12[0], 1)
    on(V, e12)
    V.tensor_scalar(T.H15[:], T.oneh[:], T.psH[:, 15:16], None, A.mult).then_inc(e13[0], 1)
    for k in range(0, 128, SW):
        V.tensor_copy(T.Hs[:, k:k + SW], T.psH[:, 0:SW]).then_inc(e14[0], 1)
    c1 = 2 * FIRST // 16
    parts = ((T.psC, 0, c1), (T.psD, c1, 128))
    on(P, e13)
    for ps, a, b in parts:
        P.matmul(ps[:, 0:b - a], T.H15[:], T.T2[:, a:b], True, False)
    on(P, e14)
    ready = []
    for ps, a, b in parts:
        e, f = new(1), new(1)
        P.matmul(ps[:, 0:b - a], T.Hs[:], T.I16[:, a:b], False, True).then_inc(e[0], 1)
        on(V, e)
        V.tensor_copy(T.off[:, a:b], ps[:, 0:b - a]).then_inc(f[0], 1)
        ready.append(f)

    W = nw * J + 4
    for k, (o, w) in enumerate(((0, FIRST), (2 * FIRST, Q // 2 - FIRST))):
        e = new(2)
        for q in (V, S):
            on(q, ready[k])
            if k == 0:
                q.wait_ge(T.sem.s_w, 16)
                q.wait_ge(T.sem.x_in, x_all)
        V.tensor_copy(T.yb[:, o:o + w], T.win[:, 0:W].indirect(T.off[:, o // 16:(o + w) // 16])).then_inc(e[0], 1)
        S.activation(T.yb[:, o + w:o + 2 * w], T.win[:, 0:W].indirect(T.off[:, (o + w) // 16:(o + 2 * w) // 16]), F.Copy,
                     bias=-0.0).then_inc(e[0], 1)
        on(g.sync, e)
        g.sync.dma_start(T.y[:, o:o + 2 * w], T.yb[:, o:o + 2 * w]).then_inc(T.sem.s_y, 16)
    g.sync.wait_ge(T.sem.s_y, 32)
    g.wait_ge(T.sem.ls, sent)
